import numpy as np
CORES = [0,1]
N = 2
def setup_inputs(rng):
    return {"x": rng.standard_normal((N, 128, 64), dtype=np.float32)}
def reference(x):
    b = 64 // N
    blocks = x.reshape(N, 128, N, b)
    return {"y": np.ascontiguousarray(blocks.transpose(2, 1, 0, 3)).reshape(N, 128, 64)}

SCRATCH = {
    "send": ("sbuf", [128, 32], "float32"),
    "land": ("sbuf", [128, 32], "float32"),
}
SEMAPHORES = ["loaded", "kept", "sent", "arrived", "stored"]


def rank_program(g, core, T, topo):
    rank = T.rank_of(core)
    if rank is None:
        return
    n = len(T.cores)
    b = T.x.shape[1] // n
    peer_rank = 1 - rank
    peer = T.cores[peer_rank]
    mine = slice(rank * b, (rank + 1) * b)
    theirs = slice(peer_rank * b, (peer_rank + 1) * b)

    g.scalar.dma_start(T.send[:], T.x[:, theirs]).then_inc(T.sem.loaded, 16)
    g.sync.dma_start(T.y[:, mine], T.x[:, mine]).then_inc(T.sem.kept, 16)

    rid, pid, _se = topo.addr(peer)
    g.wait_ge(T.sem.loaded, 16)
    g.remote_dma(T.land[:], T.send[:], T.sem.arrived, T.sem.sent, pid, rid, topo.mask(core, peer))

    g.sync.wait_ge(T.sem.arrived, 16)
    g.sync.dma_start(T.y[:, theirs], T.land[:]).then_inc(T.sem.stored, 16)

    g.wait_ge(T.sem.sent, 16)
    g.wait_ge(T.sem.kept, 16)
    g.wait_ge(T.sem.stored, 16)
